import numpy as np
import ml_dtypes


def mxq(x, axis, fmt="e4m3"):
    dtype, down = {"e4m3": (ml_dtypes.float8_e4m3fn, 7), "e5m2": (ml_dtypes.float8_e5m2, 14)}[fmt]
    v = np.moveaxis(np.asarray(x, np.float32).astype(ml_dtypes.bfloat16).astype(np.float64), axis, -1)
    blocks = v.reshape(v.shape[:-1] + (-1, 32))
    amax = np.abs(blocks).max(-1, keepdims=True)
    byte = np.maximum(np.where(amax > 0, np.frexp(amax)[1] - 1 + 127, 0) - down, 1)
    scale = np.exp2(byte - 127.0)
    codes = (blocks / scale).astype(np.float32).astype(dtype).astype(np.float64)
    return np.moveaxis((codes * scale).reshape(v.shape), -1, axis)


WIDE = False


def mx_kscale(k):
    if not WIDE:
        return np.ones(k)
    levels = np.array([10, -10, 5, -5, 0])
    if k % 512:
        return np.exp2(np.random.permutation(np.resize(levels, k // 32))).repeat(32)
    a = np.empty((k // 512, 16))
    for p in range(k // 512):
        a[p, :8] = np.random.permutation(np.resize(levels, 8))
        for g in range(8):
            far = levels[np.abs(levels - a[p, g]) >= 10]
            a[p, g + 8] = far[np.random.randint(len(far))]
    return np.exp2(a.ravel()).repeat(32)


def f64(x):
    return np.asarray(x).astype(np.float64)


def striped(idx):
    return np.tile(idx.reshape(-1, 16).T, (8, 1)).astype(np.uint16)


def unstriped(offs):
    return offs[:16].T.reshape(-1).astype(np.int64)


def silu(v):
    return v / (1.0 + np.exp(-np.maximum(v, -700.0)))


K, T, E, C, H, N = 512, 768, 12, 128, 1024, 128


def by_expert(wq, xq):
    return np.concatenate([wq[e].T @ xq[:, e * C:(e + 1) * C] for e in range(E)], axis=1)


def setup_inputs():
    n = np.random.standard_normal
    s = mx_kscale(K)[:, None]
    u = mx_kscale(H)
    first = np.random.permutation(np.repeat(np.arange(E), T // E))
    second = (first + 1 + np.random.permutation(np.repeat(np.arange(E - 1), -(-T // (E - 1)))[:T])) % E
    while np.bincount(second, minlength=E).max() != T // E:
        load = np.bincount(second, minlength=E); hi, lo = int(load.argmax()), int(load.argmin())
        t = np.flatnonzero((second == hi) & (first != lo))[0]; second[t] = lo
    slot_token = np.empty(E * C, np.int64); pos = np.empty((2, T), np.int64); fill = np.zeros(E, np.int64)
    place = np.stack([np.random.permutation(C) for _ in range(E)])
    for r, deal in enumerate((first, second)):
        for t in np.random.permutation(T):
            e = deal[t]; j = e * C + place[e, fill[e]]; fill[e] += 1; slot_token[j] = t; pos[r, t] = j
    g = np.random.uniform(0.2, 0.8, T)
    return {
        "xT": (n((K, T)) * s).astype(np.float32),
        "w1": (n((E, K, H)) / np.sqrt(K) / s[None] * u[None, None, :]).astype(np.float32),
        "w2": (n((E, H, N)) / np.sqrt(H) / u[None, :, None]).astype(np.float32),
        "gate": np.stack([np.tile(g, (N, 1)), np.tile(1.0 - g, (N, 1))]).astype(np.float32),
        "offs": striped(slot_token),
        "pos1": striped(pos[0]),
        "pos2": striped(pos[1]),
    }


def reference(xT, w1, w2, gate, offs, pos1, pos2):
    idx = unstriped(offs)
    xq = mxq(f64(xT)[:, idx], 0, "e4m3")
    h = silu(by_expert(mxq(f64(w1), 1, "e4m3"), xq))
    y = by_expert(mxq(f64(w2), 1, "e4m3"), mxq(h, 0, "e4m3"))
    return f64(gate[0]) * y[:, unstriped(pos1)] + f64(gate[1]) * y[:, unstriped(pos2)]

@@ -1,0 +1,230 @@
+from contextlib import ExitStack
+
+import concourse.mybir as mybir
+
+K, T, E, C, H, N = 512, 768, 12, 128, 1024, 128
+FLOPS = 2 * E * C * H * (K + N)
+
+F32 = mybir.dt.float32
+BF16 = mybir.dt.bfloat16
+U32 = mybir.dt.uint32
+I32 = mybir.dt.int32
+U16 = mybir.dt.uint16
+U8 = mybir.dt.uint8
+FP8X4 = mybir.dt.float8_e4m3fn_x4
+SILU = mybir.ActivationFunctionType.Silu
+MULT = mybir.AluOpType.mult
+ADD = mybir.AluOpType.add
+
+P = 128
+J = 4
+G = H // 512
+PAIRS = E // 2
+X_CHUNK = 256
+GATHERS = (256, 256, 512, 512)
+OUT_CHUNKS = (512, 256)
+AHEAD = 4
+
+
+def tile_routed_moe_kernel(tc, xT, w1, w2, gate, offs, pos1, pos2, out):
+    nc = tc.nc
+    with ExitStack() as ctx:
+        keep = ctx.enter_context(tc.tile_pool(name="keep", bufs=1))
+        ring = ctx.enter_context(tc.tile_pool(name="ring", bufs=2))
+        psum = ctx.enter_context(tc.psum_pool(name="psum", bufs=2))
+
+        offs_t = keep.tile([P, E * C // 16], U16, name="offs_t")
+        pos1_t = keep.tile([P, T // 16], U16, name="pos1_t")
+        pos2_t = keep.tile([P, T // 16], U16, name="pos2_t")
+        gate_t = [keep.tile([P, T], F32, name="gate%d" % r) for r in range(2)]
+        y_all = keep.tile([P, E * C], F32, name="y_all")
+        warm = keep.tile([P, 2], F32, name="warm")
+
+        nc.vector.memset(warm[:], 0.0)
+        nc.scalar.activation(warm[:, 1:2], warm[:, 0:1], SILU)
+
+        w1_raw = {}
+        w2_raw = {}
+
+        def load_w1(e):
+            t = ring.tile([P, J, H], F32, name="wraw", tag="wraw", bufs=6, align_bytes=64)
+            view = w1[e].rearrange("(p j) h -> p j h", j=J)
+            if e == E - 1:
+                for g in range(G):
+                    nc.sync.dma_start(out=t[:, :, g * 512:(g + 1) * 512], in_=view[:, :, g * 512:(g + 1) * 512])
+            else:
+                nc.sync.dma_start(out=t[:], in_=view)
+            w1_raw[e] = t
+
+        def load_w2(k):
+            t = ring.tile([P, 2 * G, J, N], F32, name="vraw", tag="vraw", bufs=3, align_bytes=64)
+            nc.sync.dma_start(out=t[:], in_=w2[2 * k:2 * k + 2].rearrange("e (g p j) n -> p (e g) j n", p=P, j=J))
+            w2_raw[k] = t
+
+        nc.sync.dma_start(out=offs_t[:], in_=offs)
+        x_raw = ring.tile([P, J, T], F32, name="wraw", tag="wraw", bufs=6, align_bytes=64)
+        nc.sync.dma_start(out=x_raw[:], in_=xT.rearrange("(p j) n -> p j n", j=J))
+
+        queue = []
+        for e in range(E):
+            queue.append((load_w1, e))
+            if e % 2 == 0 and e < 8:
+                queue.append((load_w2, e // 2))
+            if e == 5:
+                queue.append((lambda i: nc.sync.dma_start(out=pos1_t[:], in_=pos1), 0))
+                queue.append((lambda i: nc.sync.dma_start(out=pos2_t[:], in_=pos2), 0))
+        queue.append((load_w2, 4))
+        queue.append((load_w2, 5))
+        queue.append((lambda r: nc.sync.dma_start(out=gate_t[r][:], in_=gate[r]), 0))
+        queue.append((lambda r: nc.sync.dma_start(out=gate_t[r][:], in_=gate[r]), 1))
+
+        def issue_loads(last_w1):
+            while queue and (last_w1 >= E - 1 or (queue[0][0] is not load_w1) or queue[0][1] <= last_w1):
+                f, arg = queue.pop(0)
+                f(arg)
+
+        issue_loads(AHEAD - 1)
+
+        x_codes = keep.tile([P, T], U32, name="x_codes", align_bytes=64)
+        x_scales = keep.tile([P, T], U8, name="x_scales", align_bytes=64)
+        nc.gpsimd.memset(x_scales[:], 0)
+        x_grouped = []
+        for b in range(T // X_CHUNK):
+            t = keep.tile([P, X_CHUNK, J], BF16, name="x_grouped%d" % b, align_bytes=64)
+            dst = t[:].rearrange("p (c i) j -> p c j i", i=4)
+            src = x_raw[:, :, b * X_CHUNK:(b + 1) * X_CHUNK].rearrange("p j (c i) -> p c j i", i=4)
+            if b == 2:
+                nc.scalar.copy(out=dst, in_=src)
+            else:
+                nc.vector.tensor_copy(out=dst, in_=src)
+            x_grouped.append(t)
+        for b in range(T // X_CHUNK):
+            s = slice(b * X_CHUNK, (b + 1) * X_CHUNK)
+            nc.vector.quantize_mx(out=x_codes[:, s].bitcast(FP8X4), scales=x_scales[:, s],
+                                  in_=x_grouped[b][:].rearrange("p n j -> p (n j)"))
+        slot_codes = {}
+        at = 0
+        for i, n in enumerate(GATHERS):
+            codes = keep.tile([P, n], U32, name="g_codes%d" % i, align_bytes=64)
+            scales = keep.tile([P, n], U8, name="g_scales%d" % i, align_bytes=64)
+            part = offs_t[:, at // 16:(at + n) // 16]
+            nc.vector.tensor_copy(out=codes[:], in_=x_codes[:].indirect(part))
+            nc.vector.tensor_copy(out=scales[:], in_=x_scales[:].indirect(part))
+            for q in range(n // C):
+                slot_codes[(at + q * C) // C] = (codes[:, q * C:(q + 1) * C], scales[:, q * C:(q + 1) * C])
+            at += n
+
+        w1_grouped = {}
+        w1_q = {}
+        w2_grouped = {}
+        w2_q = {}
+        h_grouped = {}
+        h_q = {}
+
+        def group_w1(e):
+            for g in range(G):
+                t = ring.tile([P, 4, 128, J], BF16, name="wg%d" % g, tag="wg%d" % g, bufs=2, align_bytes=64)
+                dst = t[:].rearrange("p t m j -> p m j t")
+                src = w1_raw[e][:, :, g * 512:(g + 1) * 512].rearrange("p j (m t) -> p m j t", t=4)
+                if g == 0:
+                    nc.vector.tensor_copy(out=dst, in_=src)
+                else:
+                    nc.scalar.copy(out=dst, in_=src)
+                w1_grouped[e, g] = t
+
+        def quant_w1(e):
+            for g in range(G):
+                codes = ring.tile([P, 512], U32, name="wc", tag="wc", bufs=6, align_bytes=64)
+                scales = ring.tile([P, 512], U8, name="ws", tag="ws", bufs=6, align_bytes=64)
+                nc.vector.quantize_mx(out=codes[:].bitcast(FP8X4), scales=scales[:],
+                                      in_=w1_grouped[e, g][:].rearrange("p t m j -> p (t m j)"))
+                w1_q[e, g] = (codes, scales)
+
+        def hidden(e):
+            xc, xs = slot_codes[e]
+            t = ring.tile([P, G, C, J], BF16, name="hg", tag="hg", bufs=3, align_bytes=64)
+            for g in range(G):
+                codes, scales = w1_q[e, g]
+                acc = psum.tile([P, 4, C], F32, name="acc", tag="acc", bufs=5)
+                for q in range(4):
+                    s = slice(q * 128, (q + 1) * 128)
+                    nc.tensor.matmul_mx(out=acc[:, q, :], lhsT=codes[:, s].bitcast(FP8X4), lhsT_scale=scales[:, s],
+                                        rhs=xc.bitcast(FP8X4), rhs_scale=xs, start=True, stop=True)
+                nc.scalar.activation(t[:, g, :, :], acc[:].rearrange("p t n -> p n t"), SILU)
+            h_grouped[e] = t
+
+        def quant_h(e):
+            codes = ring.tile([P, G, C], U32, name="hc", tag="hc", bufs=6, align_bytes=64)
+            scales = ring.tile([P, G, C], U8, name="hs", tag="hs", bufs=6, align_bytes=64)
+            if e == E - 1:
+                for g in range(G):
+                    nc.vector.quantize_mx(out=codes[:, g, :].bitcast(FP8X4), scales=scales[:, g, :],
+                                          in_=h_grouped[e][:, g, :, :].rearrange("p n j -> p (n j)"))
+            else:
+                nc.vector.quantize_mx(out=codes[:].rearrange("p g n -> p (g n)").bitcast(FP8X4),
+                                      scales=scales[:].rearrange("p g n -> p (g n)"),
+                                      in_=h_grouped[e][:].rearrange("p g n j -> p (g n j)"))
+            h_q[e] = (codes, scales)
+
+        def group_w2(k):
+            t = ring.tile([P, 2 * G, N, J], BF16, name="vg", tag="vg", bufs=2, align_bytes=64)
+            dst = t[:].rearrange("p g (c i) j -> p g c j i", i=4)
+            src = w2_raw[k][:].rearrange("p g j (c i) -> p g c j i", i=4)
+            nc.vector.tensor_copy(out=dst[:, 0:G], in_=src[:, 0:G])
+            for g in range(G, 2 * G):
+                nc.scalar.copy(out=dst[:, g], in_=src[:, g])
+            w2_grouped[k] = t
+
+        def quant_w2(k):
+            codes = keep.tile([P, 2 * G, N], U32, name="vc%d" % k, align_bytes=64)
+            scales = keep.tile([P, 2 * G, N], U8, name="vs%d" % k, align_bytes=64)
+            nc.vector.quantize_mx(out=codes[:].rearrange("p g n -> p (g n)").bitcast(FP8X4),
+                                  scales=scales[:].rearrange("p g n -> p (g n)"),
+                                  in_=w2_grouped[k][:].rearrange("p g n j -> p (g n j)"))
+            w2_q[k] = (codes, scales)
+
+        def second(e):
+            wc, ws = w2_q[e // 2]
+            hc, hs = h_q[e]
+            acc = psum.tile([N, C], F32, name="acc_y", tag="acc_y", bufs=3)
+            for g in range(G):
+                r = G * (e % 2) + g
+                nc.tensor.matmul_mx(out=acc[:], lhsT=wc[:, r, :].bitcast(FP8X4), lhsT_scale=ws[:, r, :],
+                                    rhs=hc[:, g, :].bitcast(FP8X4), rhs_scale=hs[:, g, :],
+                                    start=(g == 0), stop=(g == G - 1))
+            nc.scalar.copy(out=y_all[:, e * C:(e + 1) * C], in_=acc[:])
+
+        for s in range(E + 2):
+            issue_loads(s + AHEAD)
+            if s < E:
+                group_w1(s)
+            if s % 2 == 0 and s < 8:
+                group_w2(s // 2)
+            if 1 <= s <= E:
+                quant_w1(s - 1)
+                hidden(s - 1)
+            if s % 2 == 1 and s < 8:
+                quant_w2(s // 2)
+            if s >= 2:
+                quant_h(s - 2)
+                if s - 2 < 8:
+                    second(s - 2)
+        for k in range(4, PAIRS):
+            group_w2(k)
+        for k in range(4, PAIRS):
+            quant_w2(k)
+            second(2 * k)
+            second(2 * k + 1)
+
+        at = 0
+        for i, n in enumerate(OUT_CHUNKS):
+            s = slice(at, at + n)
+            part = slice(at // 16, (at + n) // 16)
+            a = keep.tile([P, n], F32, name="first%d" % i, align_bytes=64)
+            b = keep.tile([P, n], F32, name="second%d" % i, align_bytes=64)
+            r = keep.tile([P, n], F32, name="result%d" % i, align_bytes=64)
+            nc.vector.tensor_tensor(a[:], y_all[:].indirect(pos1_t[:, part]), gate_t[0][:, s], MULT)
+            nc.vector.tensor_tensor(b[:], y_all[:].indirect(pos2_t[:, part]), gate_t[1][:, s], MULT)
+            nc.vector.tensor_tensor(r[:], a[:], b[:], ADD)
+            nc.sync.dma_start(out=out[:, s], in_=r[:])
+            at += n

@@ -22,8 +22,10 @@ G = H // 512
 PAIRS = E // 2
 X_CHUNK = 256
 GATHERS = (256, 256, 512, 512)
+V_SHARE = [(128, 0)] * 8 + [(128, 32)] * 3 + [(96, 64)]
+Y_BANKS = ((0, 1, 2, 3), (4, 5, 6, 7), (8, 9), (10, 11))
 OUT_CHUNKS = (512, 256)
-AHEAD = 4
+AHEAD = 5
 
 
 def tile_routed_moe_kernel(tc, xT, w1, w2, gate, offs, pos1, pos2, out):
@@ -49,8 +51,8 @@ def tile_routed_moe_kernel(tc, xT, w1, w2, gate, offs, pos1, pos2, out):
         def load_w1(e):
             t = ring.tile([P, J, H], F32, name="wraw", tag="wraw", bufs=6, align_bytes=64)
             view = w1[e].rearrange("(p j) h -> p j h", j=J)
-            if e == E - 1:
-                for g in range(G):
+            if e == E - 1 or e == 0:
+                for g in (1, 0):
                     nc.sync.dma_start(out=t[:, :, g * 512:(g + 1) * 512], in_=view[:, :, g * 512:(g + 1) * 512])
             else:
                 nc.sync.dma_start(out=t[:], in_=view)
@@ -61,13 +63,15 @@ def tile_routed_moe_kernel(tc, xT, w1, w2, gate, offs, pos1, pos2, out):
             nc.sync.dma_start(out=t[:], in_=w2[2 * k:2 * k + 2].rearrange("e (g p j) n -> p (e g) j n", p=P, j=J))
             w2_raw[k] = t
 
+        load_w1(0)
         nc.sync.dma_start(out=offs_t[:], in_=offs)
         x_raw = ring.tile([P, J, T], F32, name="wraw", tag="wraw", bufs=6, align_bytes=64)
         nc.sync.dma_start(out=x_raw[:], in_=xT.rearrange("(p j) n -> p j n", j=J))
 
         queue = []
         for e in range(E):
-            queue.append((load_w1, e))
+            if e > 0:
+                queue.append((load_w1, e))
             if e % 2 == 0 and e < 8:
                 queue.append((load_w2, e // 2))
             if e == 5:
@@ -88,9 +92,14 @@ def tile_routed_moe_kernel(tc, xT, w1, w2, gate, offs, pos1, pos2, out):
         x_codes = keep.tile([P, T], U32, name="x_codes", align_bytes=64)
         x_scales = keep.tile([P, T], U8, name="x_scales", align_bytes=64)
         nc.gpsimd.memset(x_scales[:], 0)
+        def first_ring(shape, dtype):
+            return ring.tile(shape, dtype, name="first", tag="first", bufs=3, align_bytes=64)
+
+        w1_first = {}
+        x_tiles = [ring.tile([P, X_CHUNK, J], BF16, name="hg", tag="hg", bufs=4, align_bytes=64) for b in range(3)]
         x_grouped = []
         for b in range(T // X_CHUNK):
-            t = keep.tile([P, X_CHUNK, J], BF16, name="x_grouped%d" % b, align_bytes=64)
+            t = x_tiles[b]
             dst = t[:].rearrange("p (c i) j -> p c j i", i=4)
             src = x_raw[:, :, b * X_CHUNK:(b + 1) * X_CHUNK].rearrange("p j (c i) -> p c j i", i=4)
             if b == 2:
@@ -121,58 +130,69 @@ def tile_routed_moe_kernel(tc, xT, w1, w2, gate, offs, pos1, pos2, out):
         h_grouped = {}
         h_q = {}
 
+        late_codes = {}
+
         def group_w1(e):
-            for g in range(G):
-                t = ring.tile([P, 4, 128, J], BF16, name="wg%d" % g, tag="wg%d" % g, bufs=2, align_bytes=64)
-                dst = t[:].rearrange("p t m j -> p m j t")
+            w1_first[e] = first_ring([P, 4, 128, J], BF16)
+            second_half = ring.tile([P, 4, 128, J], BF16, name="wg1", tag="wg1", bufs=3, align_bytes=64)
+            w1_grouped[e] = (w1_first[e], second_half)
+            for g in (1, 0):
+                dst = w1_grouped[e][g][:].rearrange("p t m j -> p m j t")
                 src = w1_raw[e][:, :, g * 512:(g + 1) * 512].rearrange("p j (m t) -> p m j t", t=4)
-                if g == 0:
-                    nc.vector.tensor_copy(out=dst, in_=src)
-                else:
-                    nc.scalar.copy(out=dst, in_=src)
-                w1_grouped[e, g] = t
+                m = V_SHARE[e][g]
+                if m > 0:
+                    nc.vector.tensor_copy(out=dst[:, 0:m], in_=src[:, 0:m])
+                if m < 128:
+                    nc.scalar.copy(out=dst[:, m:128], in_=src[:, m:128])
 
-        def quant_w1(e):
-            for g in range(G):
-                codes = ring.tile([P, 512], U32, name="wc", tag="wc", bufs=6, align_bytes=64)
-                scales = ring.tile([P, 512], U8, name="ws", tag="ws", bufs=6, align_bytes=64)
-                nc.vector.quantize_mx(out=codes[:].bitcast(FP8X4), scales=scales[:],
-                                      in_=w1_grouped[e, g][:].rearrange("p t m j -> p (t m j)"))
-                w1_q[e, g] = (codes, scales)
+        def quant_w1(e, g):
+            if g == 1 and e in late_codes:
+                codes = late_codes[e][:, 0:512]
+            else:
+                codes = ring.tile([P, 512], U32, name="wc", tag="wc", bufs=5, align_bytes=64)[:]
+            scales = ring.tile([P, 512], U8, name="ws", tag="ws", bufs=8, align_bytes=64)[:]
+            nc.vector.quantize_mx(out=codes.bitcast(FP8X4), scales=scales,
+                                  in_=w1_grouped[e][g][:].rearrange("p t m j -> p (t m j)"))
+            w1_q[e, g] = (codes, scales)
 
-        def hidden(e):
+        def hidden(e, g):
             xc, xs = slot_codes[e]
-            t = ring.tile([P, G, C, J], BF16, name="hg", tag="hg", bufs=3, align_bytes=64)
-            for g in range(G):
-                codes, scales = w1_q[e, g]
-                acc = psum.tile([P, 4, C], F32, name="acc", tag="acc", bufs=5)
-                for q in range(4):
-                    s = slice(q * 128, (q + 1) * 128)
-                    nc.tensor.matmul_mx(out=acc[:, q, :], lhsT=codes[:, s].bitcast(FP8X4), lhsT_scale=scales[:, s],
-                                        rhs=xc.bitcast(FP8X4), rhs_scale=xs, start=True, stop=True)
-                nc.scalar.activation(t[:, g, :, :], acc[:].rearrange("p t n -> p n t"), SILU)
-            h_grouped[e] = t
+            if e not in h_grouped:
+                h_grouped[e] = ring.tile([P, G, C, J], BF16, name="hg", tag="hg", bufs=4, align_bytes=64)
+            codes, scales = w1_q[e, g]
+            acc = psum.tile([P, 4, C], F32, name="acc", tag="acc", bufs=4)
+            for q in range(4):
+                s = slice(q * 128, (q + 1) * 128)
+                nc.tensor.matmul_mx(out=acc[:, q, :], lhsT=codes[:, s].bitcast(FP8X4), lhsT_scale=scales[:, s],
+                                    rhs=xc.bitcast(FP8X4), rhs_scale=xs, start=True, stop=True)
+            nc.scalar.activation(h_grouped[e][:, g, :, :], acc[:].rearrange("p t n -> p n t"), SILU)
 
         def quant_h(e):
-            codes = ring.tile([P, G, C], U32, name="hc", tag="hc", bufs=6, align_bytes=64)
-            scales = ring.tile([P, G, C], U8, name="hs", tag="hs", bufs=6, align_bytes=64)
-            if e == E - 1:
-                for g in range(G):
-                    nc.vector.quantize_mx(out=codes[:, g, :].bitcast(FP8X4), scales=scales[:, g, :],
-                                          in_=h_grouped[e][:, g, :, :].rearrange("p n j -> p (n j)"))
+            if e <= 6:
+                codes = late_codes[e + 1][:, 512:768]
             else:
-                nc.vector.quantize_mx(out=codes[:].rearrange("p g n -> p (g n)").bitcast(FP8X4),
-                                      scales=scales[:].rearrange("p g n -> p (g n)"),
-                                      in_=h_grouped[e][:].rearrange("p g n j -> p (g n j)"))
+                codes = ring.tile([P, G * C], U32, name="hc", tag="hc", bufs=5, align_bytes=64)[:]
+            scales = ring.tile([P, G * C], U8, name="hs", tag="hs", bufs=7, align_bytes=64)[:]
+            parts = ((0, 1), (1, 2)) if e == E - 1 else ((0, 2),)
+            for a, b in parts:
+                nc.vector.quantize_mx(out=codes[:, a * C:b * C].bitcast(FP8X4), scales=scales[:, a * C:b * C],
+                                      in_=h_grouped[e][:, a:b, :, :].rearrange("p g n j -> p (g n j)"))
             h_q[e] = (codes, scales)
 
         def group_w2(k):
             t = ring.tile([P, 2 * G, N, J], BF16, name="vg", tag="vg", bufs=2, align_bytes=64)
             dst = t[:].rearrange("p g (c i) j -> p g c j i", i=4)
             src = w2_raw[k][:].rearrange("p g j (c i) -> p g c j i", i=4)
-            nc.vector.tensor_copy(out=dst[:, 0:G], in_=src[:, 0:G])
-            for g in range(G, 2 * G):
-                nc.scalar.copy(out=dst[:, g], in_=src[:, g])
+            if k == 0:
+                for g in range(2 * G):
+                    nc.scalar.copy(out=dst[:, g], in_=src[:, g])
+            else:
+                nc.vector.tensor_copy(out=dst[:, 0:G], in_=src[:, 0:G])
+                if k < 4:
+                    nc.vector.tensor_copy(out=dst[:, G:2 * G], in_=src[:, G:2 * G])
+                else:
+                    for g in range(G, 2 * G):
+                        nc.scalar.copy(out=dst[:, g], in_=src[:, g])
             w2_grouped[k] = t
 
         def quant_w2(k):
@@ -183,38 +203,52 @@ def tile_routed_moe_kernel(tc, xT, w1, w2, gate, offs, pos1, pos2, out):
                                   in_=w2_grouped[k][:].rearrange("p g n j -> p (g n j)"))
             w2_q[k] = (codes, scales)
 
+        y_bank = {}
+
         def second(e):
             wc, ws = w2_q[e // 2]
             hc, hs = h_q[e]
-            acc = psum.tile([N, C], F32, name="acc_y", tag="acc_y", bufs=3)
+            bank = [b for b in Y_BANKS if e in b][0]
+            if e == bank[0]:
+                y_bank[bank] = psum.tile([N, 4, C], F32, name="acc_y", tag="acc_y", bufs=4)
+            acc = y_bank[bank]
             for g in range(G):
                 r = G * (e % 2) + g
-                nc.tensor.matmul_mx(out=acc[:], lhsT=wc[:, r, :].bitcast(FP8X4), lhsT_scale=ws[:, r, :],
-                                    rhs=hc[:, g, :].bitcast(FP8X4), rhs_scale=hs[:, g, :],
+                s = slice(g * C, (g + 1) * C)
+                nc.tensor.matmul_mx(out=acc[:, e - bank[0], :], lhsT=wc[:, r, :].bitcast(FP8X4), lhsT_scale=ws[:, r, :],
+                                    rhs=hc[:, s].bitcast(FP8X4), rhs_scale=hs[:, s],
                                     start=(g == 0), stop=(g == G - 1))
-            nc.scalar.copy(out=y_all[:, e * C:(e + 1) * C], in_=acc[:])
+            if e == bank[-1]:
+                n = len(bank)
+                nc.scalar.copy(out=y_all[:, bank[0] * C:(e + 1) * C], in_=acc[:, 0:n, :].rearrange("p a n -> p (a n)"))
 
-        for s in range(E + 2):
-            issue_loads(s + AHEAD)
+        for s in range(E + 3):
+            issue_loads(min(s, E - 1) + AHEAD - 1)
             if s < E:
                 group_w1(s)
             if s % 2 == 0 and s < 8:
                 group_w2(s // 2)
-            if 1 <= s <= E:
-                quant_w1(s - 1)
-                hidden(s - 1)
+            if s < E:
+                quant_w1(s, 0)
+                hidden(s, 0)
+            if 2 <= s < E:
+                late_codes[s - 2] = first_ring([P, 768], U32)
+            if 0 <= s - 2 < E:
+                quant_w1(s - 2, 1)
+                hidden(s - 2, 1)
             if s % 2 == 1 and s < 8:
                 quant_w2(s // 2)
-            if s >= 2:
-                quant_h(s - 2)
-                if s - 2 < 8:
-                    second(s - 2)
+            if 0 <= s - 3 < E - 2:
+                quant_h(s - 3)
+            if 0 <= s - 3 < 8:
+                second(s - 3)
         for k in range(4, PAIRS):
             group_w2(k)
-        for k in range(4, PAIRS):
             quant_w2(k)
-            second(2 * k)
-            second(2 * k + 1)
+        quant_h(E - 2)
+        quant_h(E - 1)
+        for e in range(8, E):
+            second(e)
 
         at = 0
         for i, n in enumerate(OUT_CHUNKS):

@@ -19,13 +19,15 @@ ADD = mybir.AluOpType.add
 P = 128
 J = 4
 G = H // 512
-PAIRS = E // 2
 X_CHUNK = 256
 GATHERS = (256, 256, 512, 512)
-V_SHARE = [(128, 0)] * 8 + [(128, 32)] * 3 + [(96, 64)]
-Y_BANKS = ((0, 1, 2, 3), (4, 5, 6, 7), (8, 9), (10, 11))
+V_SHARE = [(96, 0)] * 2 + [(128, 0), (128, 16), (128, 16), (128, 0), (128, 0), (128, 32), (112, 16), (96, 64), (112, 64), (128, 32)]
+Y_BANKS = ((0, 1, 2, 3), (4, 5, 6, 7), (8, 9, 10), (11,))
+W2_GROUPS = ((0, 1), (2, 3), (4, 5), (6, 7), (8, 9), (10,), (11,))
+W2_SHARE = (2, 3, 3, 3, 4, 2, 1)
+GROUPS = ((0,), (1,), (2, 3), (4, 5), (6, 7), (8, 9), (10,), (11,))
 OUT_CHUNKS = (512, 256)
-AHEAD = 5
+W2_AHEAD = 4
 
 
 def tile_routed_moe_kernel(tc, xT, w1, w2, gate, offs, pos1, pos2, out):
@@ -38,7 +40,7 @@ def tile_routed_moe_kernel(tc, xT, w1, w2, gate, offs, pos1, pos2, out):
         offs_t = keep.tile([P, E * C // 16], U16, name="offs_t")
         pos1_t = keep.tile([P, T // 16], U16, name="pos1_t")
         pos2_t = keep.tile([P, T // 16], U16, name="pos2_t")
-        gate_t = [keep.tile([P, T], F32, name="gate%d" % r) for r in range(2)]
+        gate_t = {}
         y_all = keep.tile([P, E * C], F32, name="y_all")
         warm = keep.tile([P, 2], F32, name="warm")
 
@@ -48,55 +50,34 @@ def tile_routed_moe_kernel(tc, xT, w1, w2, gate, offs, pos1, pos2, out):
         w1_raw = {}
         w2_raw = {}
 
-        def load_w1(e):
-            t = ring.tile([P, J, H], F32, name="wraw", tag="wraw", bufs=6, align_bytes=64)
-            view = w1[e].rearrange("(p j) h -> p j h", j=J)
-            if e == E - 1 or e == 0:
-                for g in (1, 0):
-                    nc.sync.dma_start(out=t[:, :, g * 512:(g + 1) * 512], in_=view[:, :, g * 512:(g + 1) * 512])
-            else:
-                nc.sync.dma_start(out=t[:], in_=view)
-            w1_raw[e] = t
+        def raw_tile(shape):
+            return ring.tile(shape, F32, name="raw", tag="raw", bufs=3, align_bytes=64)
+
+        def load_w1(group):
+            n = len(group)
+            t = raw_tile([P, n, J, H])
+            view = w1[group[0]:group[0] + n].rearrange("e (p j) h -> p e j h", j=J)
+            nc.sync.dma_start(out=t[:], in_=view)
+            for e in group:
+                w1_raw[e] = t[:, e - group[0]]
 
         def load_w2(k):
-            t = ring.tile([P, 2 * G, J, N], F32, name="vraw", tag="vraw", bufs=3, align_bytes=64)
-            nc.sync.dma_start(out=t[:], in_=w2[2 * k:2 * k + 2].rearrange("e (g p j) n -> p (e g) j n", p=P, j=J))
+            group = W2_GROUPS[k]
+            n = len(group)
+            t = ring.tile([P, n * G, J, N], F32, name="vraw", tag="vraw", bufs=W2_AHEAD, align_bytes=64)
+            nc.sync.dma_start(out=t[:], in_=w2[group[0]:group[0] + n].rearrange("e (g p j) n -> p (e g) j n", p=P, j=J))
             w2_raw[k] = t
 
-        load_w1(0)
         nc.sync.dma_start(out=offs_t[:], in_=offs)
-        x_raw = ring.tile([P, J, T], F32, name="wraw", tag="wraw", bufs=6, align_bytes=64)
+        x_raw = raw_tile([P, J, T])
         nc.sync.dma_start(out=x_raw[:], in_=xT.rearrange("(p j) n -> p j n", j=J))
-
-        queue = []
-        for e in range(E):
-            if e > 0:
-                queue.append((load_w1, e))
-            if e % 2 == 0 and e < 8:
-                queue.append((load_w2, e // 2))
-            if e == 5:
-                queue.append((lambda i: nc.sync.dma_start(out=pos1_t[:], in_=pos1), 0))
-                queue.append((lambda i: nc.sync.dma_start(out=pos2_t[:], in_=pos2), 0))
-        queue.append((load_w2, 4))
-        queue.append((load_w2, 5))
-        queue.append((lambda r: nc.sync.dma_start(out=gate_t[r][:], in_=gate[r]), 0))
-        queue.append((lambda r: nc.sync.dma_start(out=gate_t[r][:], in_=gate[r]), 1))
-
-        def issue_loads(last_w1):
-            while queue and (last_w1 >= E - 1 or (queue[0][0] is not load_w1) or queue[0][1] <= last_w1):
-                f, arg = queue.pop(0)
-                f(arg)
-
-        issue_loads(AHEAD - 1)
+        load_w1(GROUPS[0])
+        load_w1(GROUPS[1])
 
         x_codes = keep.tile([P, T], U32, name="x_codes", align_bytes=64)
         x_scales = keep.tile([P, T], U8, name="x_scales", align_bytes=64)
         nc.gpsimd.memset(x_scales[:], 0)
-        def first_ring(shape, dtype):
-            return ring.tile(shape, dtype, name="first", tag="first", bufs=3, align_bytes=64)
-
-        w1_first = {}
-        x_tiles = [ring.tile([P, X_CHUNK, J], BF16, name="hg", tag="hg", bufs=4, align_bytes=64) for b in range(3)]
+        x_tiles = [ring.tile([P, X_CHUNK, J], BF16, name="hg", tag="hg", bufs=3, align_bytes=64) for b in range(3)]
         x_grouped = []
         for b in range(T // X_CHUNK):
             t = x_tiles[b]
@@ -130,12 +111,8 @@ def tile_routed_moe_kernel(tc, xT, w1, w2, gate, offs, pos1, pos2, out):
         h_grouped = {}
         h_q = {}
 
-        late_codes = {}
-
         def group_w1(e):
-            w1_first[e] = first_ring([P, 4, 128, J], BF16)
-            second_half = ring.tile([P, 4, 128, J], BF16, name="wg1", tag="wg1", bufs=3, align_bytes=64)
-            w1_grouped[e] = (w1_first[e], second_half)
+            w1_grouped[e] = [ring.tile([P, 4, 128, J], BF16, name="wg", tag="wg", bufs=5, align_bytes=64) for g in range(G)]
             for g in (1, 0):
                 dst = w1_grouped[e][g][:].rearrange("p t m j -> p m j t")
                 src = w1_raw[e][:, :, g * 512:(g + 1) * 512].rearrange("p j (m t) -> p m j t", t=4)
@@ -146,119 +123,115 @@ def tile_routed_moe_kernel(tc, xT, w1, w2, gate, offs, pos1, pos2, out):
                     nc.scalar.copy(out=dst[:, m:128], in_=src[:, m:128])
 
         def quant_w1(e, g):
-            if g == 1 and e in late_codes:
-                codes = late_codes[e][:, 0:512]
-            else:
-                codes = ring.tile([P, 512], U32, name="wc", tag="wc", bufs=5, align_bytes=64)[:]
-            scales = ring.tile([P, 512], U8, name="ws", tag="ws", bufs=8, align_bytes=64)[:]
+            codes = ring.tile([P, 512], U32, name="wc", tag="wc", bufs=6, align_bytes=64)[:]
+            scales = ring.tile([P, 512], U8, name="ws", tag="ws", bufs=6, align_bytes=64)[:]
             nc.vector.quantize_mx(out=codes.bitcast(FP8X4), scales=scales,
                                   in_=w1_grouped[e][g][:].rearrange("p t m j -> p (t m j)"))
             w1_q[e, g] = (codes, scales)
 
         def hidden(e, g):
             xc, xs = slot_codes[e]
-            if e not in h_grouped:
-                h_grouped[e] = ring.tile([P, G, C, J], BF16, name="hg", tag="hg", bufs=4, align_bytes=64)
+            group = [b for b in GROUPS if e in b][0]
+            if group not in h_grouped:
+                h_grouped[group] = ring.tile([P, 2, G, C, J], BF16, name="hg", tag="hg", bufs=3, align_bytes=64)
             codes, scales = w1_q[e, g]
             acc = psum.tile([P, 4, C], F32, name="acc", tag="acc", bufs=4)
             for q in range(4):
                 s = slice(q * 128, (q + 1) * 128)
                 nc.tensor.matmul_mx(out=acc[:, q, :], lhsT=codes[:, s].bitcast(FP8X4), lhsT_scale=scales[:, s],
                                     rhs=xc.bitcast(FP8X4), rhs_scale=xs, start=True, stop=True)
-            nc.scalar.activation(h_grouped[e][:, g, :, :], acc[:].rearrange("p t n -> p n t"), SILU)
+            nc.scalar.activation(h_grouped[group][:, e - group[0], g, :, :], acc[:].rearrange("p t n -> p n t"), SILU)
 
-        def quant_h(e):
-            if e <= 6:
-                codes = late_codes[e + 1][:, 512:768]
-            else:
-                codes = ring.tile([P, G * C], U32, name="hc", tag="hc", bufs=5, align_bytes=64)[:]
-            scales = ring.tile([P, G * C], U8, name="hs", tag="hs", bufs=7, align_bytes=64)[:]
-            parts = ((0, 1), (1, 2)) if e == E - 1 else ((0, 2),)
-            for a, b in parts:
-                nc.vector.quantize_mx(out=codes[:, a * C:b * C].bitcast(FP8X4), scales=scales[:, a * C:b * C],
-                                      in_=h_grouped[e][:, a:b, :, :].rearrange("p g n j -> p (g n j)"))
-            h_q[e] = (codes, scales)
+        def quant_h(group):
+            n = len(group)
+            codes = keep.tile([P, n, G * C], U32, name="hc%d" % group[0], align_bytes=64)
+            scales = keep.tile([P, n, G * C], U8, name="hs%d" % group[0], align_bytes=64)
+            nc.vector.quantize_mx(out=codes[:].rearrange("p e n -> p (e n)").bitcast(FP8X4),
+                                  scales=scales[:].rearrange("p e n -> p (e n)"),
+                                  in_=h_grouped[group][:, 0:n].rearrange("p e g n j -> p (e g n j)"))
+            for e in group:
+                h_q[e] = (codes[:, e - group[0]], scales[:, e - group[0]])
 
         def group_w2(k):
-            t = ring.tile([P, 2 * G, N, J], BF16, name="vg", tag="vg", bufs=2, align_bytes=64)
+            total = len(W2_GROUPS[k]) * G
+            t = ring.tile([P, total, N, J], BF16, name="vg", tag="vg", bufs=2, align_bytes=64)
             dst = t[:].rearrange("p g (c i) j -> p g c j i", i=4)
             src = w2_raw[k][:].rearrange("p g j (c i) -> p g c j i", i=4)
-            if k == 0:
-                for g in range(2 * G):
-                    nc.scalar.copy(out=dst[:, g], in_=src[:, g])
-            else:
-                nc.vector.tensor_copy(out=dst[:, 0:G], in_=src[:, 0:G])
-                if k < 4:
-                    nc.vector.tensor_copy(out=dst[:, G:2 * G], in_=src[:, G:2 * G])
-                else:
-                    for g in range(G, 2 * G):
-                        nc.scalar.copy(out=dst[:, g], in_=src[:, g])
+            n = W2_SHARE[k]
+            nc.vector.tensor_copy(out=dst[:, 0:n], in_=src[:, 0:n])
+            for g in range(n, total):
+                nc.scalar.copy(out=dst[:, g], in_=src[:, g])
             w2_grouped[k] = t
 
         def quant_w2(k):
-            codes = keep.tile([P, 2 * G, N], U32, name="vc%d" % k, align_bytes=64)
-            scales = keep.tile([P, 2 * G, N], U8, name="vs%d" % k, align_bytes=64)
+            total = len(W2_GROUPS[k]) * G
+            codes = ring.tile([P, total, N], U32, name="vc", tag="vc", bufs=2, align_bytes=64)
+            scales = ring.tile([P, total, N], U8, name="vs", tag="vs", bufs=2, align_bytes=64)
             nc.vector.quantize_mx(out=codes[:].rearrange("p g n -> p (g n)").bitcast(FP8X4),
                                   scales=scales[:].rearrange("p g n -> p (g n)"),
                                   in_=w2_grouped[k][:].rearrange("p g n j -> p (g n j)"))
-            w2_q[k] = (codes, scales)
+            for i, e in enumerate(W2_GROUPS[k]):
+                w2_q[e] = (codes[:, i * G:(i + 1) * G], scales[:, i * G:(i + 1) * G])
 
         y_bank = {}
 
         def second(e):
-            wc, ws = w2_q[e // 2]
+            wc, ws = w2_q[e]
             hc, hs = h_q[e]
             bank = [b for b in Y_BANKS if e in b][0]
             if e == bank[0]:
                 y_bank[bank] = psum.tile([N, 4, C], F32, name="acc_y", tag="acc_y", bufs=4)
             acc = y_bank[bank]
             for g in range(G):
-                r = G * (e % 2) + g
                 s = slice(g * C, (g + 1) * C)
-                nc.tensor.matmul_mx(out=acc[:, e - bank[0], :], lhsT=wc[:, r, :].bitcast(FP8X4), lhsT_scale=ws[:, r, :],
+                nc.tensor.matmul_mx(out=acc[:, e - bank[0], :], lhsT=wc[:, g, :].bitcast(FP8X4), lhsT_scale=ws[:, g, :],
                                     rhs=hc[:, s].bitcast(FP8X4), rhs_scale=hs[:, s],
                                     start=(g == 0), stop=(g == G - 1))
             if e == bank[-1]:
                 n = len(bank)
-                nc.scalar.copy(out=y_all[:, bank[0] * C:(e + 1) * C], in_=acc[:, 0:n, :].rearrange("p a n -> p (a n)"))
+                dst = y_all[:, bank[0] * C:(e + 1) * C]
+                src = acc[:, 0:n, :].rearrange("p a n -> p (a n)")
+                if e == E - 1:
+                    nc.vector.tensor_copy(out=dst, in_=src)
+                else:
+                    nc.scalar.copy(out=dst, in_=src)
 
-        for s in range(E + 3):
-            issue_loads(min(s, E - 1) + AHEAD - 1)
-            if s < E:
-                group_w1(s)
-            if s % 2 == 0 and s < 8:
-                group_w2(s // 2)
-            if s < E:
-                quant_w1(s, 0)
-                hidden(s, 0)
-            if 2 <= s < E:
-                late_codes[s - 2] = first_ring([P, 768], U32)
-            if 0 <= s - 2 < E:
-                quant_w1(s - 2, 1)
-                hidden(s - 2, 1)
-            if s % 2 == 1 and s < 8:
-                quant_w2(s // 2)
-            if 0 <= s - 3 < E - 2:
-                quant_h(s - 3)
-            if 0 <= s - 3 < 8:
-                second(s - 3)
-        for k in range(4, PAIRS):
+        for i, group in enumerate(GROUPS):
+            if i + 2 < len(GROUPS):
+                load_w1(GROUPS[i + 2])
+            if i == 2:
+                nc.sync.dma_start(out=pos1_t[:], in_=pos1)
+                nc.sync.dma_start(out=pos2_t[:], in_=pos2)
+            if i + 2 == len(GROUPS) - 1:
+                for k in range(W2_AHEAD):
+                    load_w2(k)
+            for e in group:
+                group_w1(e)
+            for e in group:
+                for g in range(G):
+                    quant_w1(e, g)
+                    hidden(e, g)
+            quant_h(group)
+        for k in range(len(W2_GROUPS)):
             group_w2(k)
+            if k + W2_AHEAD < len(W2_GROUPS):
+                load_w2(k + W2_AHEAD)
+            if k + W2_AHEAD == len(W2_GROUPS) - 1:
+                for r in range(2):
+                    gate_t[r] = raw_tile([P, T])
+                    nc.sync.dma_start(out=gate_t[r][:], in_=gate[r])
             quant_w2(k)
-        quant_h(E - 2)
-        quant_h(E - 1)
-        for e in range(8, E):
-            second(e)
+            for e in W2_GROUPS[k]:
+                second(e)
 
         at = 0
         for i, n in enumerate(OUT_CHUNKS):
             s = slice(at, at + n)
             part = slice(at // 16, (at + n) // 16)
-            a = keep.tile([P, n], F32, name="first%d" % i, align_bytes=64)
-            b = keep.tile([P, n], F32, name="second%d" % i, align_bytes=64)
-            r = keep.tile([P, n], F32, name="result%d" % i, align_bytes=64)
+            a = ring.tile([P, n], F32, name="hg", tag="hg", bufs=3, align_bytes=64)
+            b = ring.tile([P, n], F32, name="hg", tag="hg", bufs=3, align_bytes=64)
             nc.vector.tensor_tensor(a[:], y_all[:].indirect(pos1_t[:, part]), gate_t[0][:, s], MULT)
             nc.vector.tensor_tensor(b[:], y_all[:].indirect(pos2_t[:, part]), gate_t[1][:, s], MULT)
-            nc.vector.tensor_tensor(r[:], a[:], b[:], ADD)
-            nc.sync.dma_start(out=out[:, s], in_=r[:])
+            nc.vector.tensor_tensor(a[:], a[:], b[:], ADD)
+            nc.sync.dma_start(out=out[:, s], in_=a[:])
             at += n

@@ -20,14 +20,15 @@ P = 128
 J = 4
 G = H // 512
 X_CHUNK = 256
-GATHERS = (256, 256, 512, 512)
-V_SHARE = [(96, 0)] * 2 + [(128, 0), (128, 16), (128, 16), (128, 0), (128, 0), (128, 32), (112, 16), (96, 64), (112, 64), (128, 32)]
+GATHERS = (512, 512, 512)
+V_SHARE = [(128, 16), (128, 0)] + [(128, 16)] * 7 + [(128, 0), (64, 64), (128, 32)]
 Y_BANKS = ((0, 1, 2, 3), (4, 5, 6, 7), (8, 9, 10), (11,))
-W2_GROUPS = ((0, 1), (2, 3), (4, 5), (6, 7), (8, 9), (10,), (11,))
-W2_SHARE = (2, 3, 3, 3, 4, 2, 1)
-GROUPS = ((0,), (1,), (2, 3), (4, 5), (6, 7), (8, 9), (10,), (11,))
+W2_SHARE = {(0, 1): 3, (2, 3): 3, (4, 5): 4, (6, 7): 2, (8, 9): 4, (10,): 1, (11,): 2}
+W1_GROUPS = ((0, 1), (2, 3), (4, 5), (6, 7), (8, 9), (10,), (11,))
+ORDER = [("w1", (0, 1)), ("w1", (2, 3)), ("w1", (4, 5)), ("w1", (6, 7)), ("w2", (0, 1)), ("w1", (8, 9)), ("w2", (2, 3)), ("w2", (4, 5)),
+         ("w1", (10,)), ("w2", (6, 7)), ("w1", (11,)), ("w2", (8, 9)), ("w2", (10,)), ("w2", (11,))]
 OUT_CHUNKS = (512, 256)
-W2_AHEAD = 4
+RAW_BUFS = 4
 
 
 def tile_routed_moe_kernel(tc, xT, w1, w2, gate, offs, pos1, pos2, out):
@@ -40,39 +41,33 @@ def tile_routed_moe_kernel(tc, xT, w1, w2, gate, offs, pos1, pos2, out):
         offs_t = keep.tile([P, E * C // 16], U16, name="offs_t")
         pos1_t = keep.tile([P, T // 16], U16, name="pos1_t")
         pos2_t = keep.tile([P, T // 16], U16, name="pos2_t")
-        gate_t = {}
         y_all = keep.tile([P, E * C], F32, name="y_all")
         warm = keep.tile([P, 2], F32, name="warm")
 
         nc.vector.memset(warm[:], 0.0)
         nc.scalar.activation(warm[:, 1:2], warm[:, 0:1], SILU)
 
-        w1_raw = {}
-        w2_raw = {}
-
         def raw_tile(shape):
-            return ring.tile(shape, F32, name="raw", tag="raw", bufs=3, align_bytes=64)
+            return ring.tile(shape, F32, name="raw", tag="raw", bufs=RAW_BUFS, align_bytes=64)
 
-        def load_w1(group):
-            n = len(group)
-            t = raw_tile([P, n, J, H])
-            view = w1[group[0]:group[0] + n].rearrange("e (p j) h -> p e j h", j=J)
-            nc.sync.dma_start(out=t[:], in_=view)
-            for e in group:
-                w1_raw[e] = t[:, e - group[0]]
-
-        def load_w2(k):
-            group = W2_GROUPS[k]
-            n = len(group)
-            t = ring.tile([P, n * G, J, N], F32, name="vraw", tag="vraw", bufs=W2_AHEAD, align_bytes=64)
-            nc.sync.dma_start(out=t[:], in_=w2[group[0]:group[0] + n].rearrange("e (g p j) n -> p (e g) j n", p=P, j=J))
-            w2_raw[k] = t
-
-        nc.sync.dma_start(out=offs_t[:], in_=offs)
         x_raw = raw_tile([P, J, T])
         nc.sync.dma_start(out=x_raw[:], in_=xT.rearrange("(p j) n -> p j n", j=J))
-        load_w1(GROUPS[0])
-        load_w1(GROUPS[1])
+        nc.sync.dma_start(out=offs_t[:], in_=offs)
+        raw = {}
+        for i, (kind, group) in enumerate(ORDER):
+            n = len(group)
+            if kind == "w1":
+                t = raw_tile([P, n, J, H])
+                nc.sync.dma_start(out=t[:], in_=w1[group[0]:group[0] + n].rearrange("e (p j) h -> p e j h", j=J))
+            else:
+                t = raw_tile([P, n * G, J, N])
+                nc.sync.dma_start(out=t[:], in_=w2[group[0]:group[0] + n].rearrange("e (g p j) n -> p (e g) j n", p=P, j=J))
+            raw[kind, group] = t
+            if i == RAW_BUFS - 2:
+                nc.sync.dma_start(out=pos1_t[:], in_=pos1)
+                nc.sync.dma_start(out=pos2_t[:], in_=pos2)
+        gate_t = raw_tile([P, 2, T])
+        nc.sync.dma_start(out=gate_t[:], in_=gate.rearrange("r p t -> p r t"))
 
         x_codes = keep.tile([P, T], U32, name="x_codes", align_bytes=64)
         x_scales = keep.tile([P, T], U8, name="x_scales", align_bytes=64)
@@ -83,7 +78,7 @@ def tile_routed_moe_kernel(tc, xT, w1, w2, gate, offs, pos1, pos2, out):
             t = x_tiles[b]
             dst = t[:].rearrange("p (c i) j -> p c j i", i=4)
             src = x_raw[:, :, b * X_CHUNK:(b + 1) * X_CHUNK].rearrange("p j (c i) -> p c j i", i=4)
-            if b == 2:
+            if b >= 1:
                 nc.scalar.copy(out=dst, in_=src)
             else:
                 nc.vector.tensor_copy(out=dst, in_=src)
@@ -106,16 +101,15 @@ def tile_routed_moe_kernel(tc, xT, w1, w2, gate, offs, pos1, pos2, out):
 
         w1_grouped = {}
         w1_q = {}
-        w2_grouped = {}
         w2_q = {}
         h_grouped = {}
         h_q = {}
 
-        def group_w1(e):
+        def group_w1(e, raw_e):
             w1_grouped[e] = [ring.tile([P, 4, 128, J], BF16, name="wg", tag="wg", bufs=5, align_bytes=64) for g in range(G)]
             for g in (1, 0):
                 dst = w1_grouped[e][g][:].rearrange("p t m j -> p m j t")
-                src = w1_raw[e][:, :, g * 512:(g + 1) * 512].rearrange("p j (m t) -> p m j t", t=4)
+                src = raw_e[:, :, g * 512:(g + 1) * 512].rearrange("p j (m t) -> p m j t", t=4)
                 m = V_SHARE[e][g]
                 if m > 0:
                     nc.vector.tensor_copy(out=dst[:, 0:m], in_=src[:, 0:m])
@@ -131,7 +125,7 @@ def tile_routed_moe_kernel(tc, xT, w1, w2, gate, offs, pos1, pos2, out):
 
         def hidden(e, g):
             xc, xs = slot_codes[e]
-            group = [b for b in GROUPS if e in b][0]
+            group = [b for b in W1_GROUPS if e in b][0]
             if group not in h_grouped:
                 h_grouped[group] = ring.tile([P, 2, G, C, J], BF16, name="hg", tag="hg", bufs=3, align_bytes=64)
             codes, scales = w1_q[e, g]
@@ -152,25 +146,21 @@ def tile_routed_moe_kernel(tc, xT, w1, w2, gate, offs, pos1, pos2, out):
             for e in group:
                 h_q[e] = (codes[:, e - group[0]], scales[:, e - group[0]])
 
-        def group_w2(k):
-            total = len(W2_GROUPS[k]) * G
+        def prepare_w2(group):
+            total = len(group) * G
             t = ring.tile([P, total, N, J], BF16, name="vg", tag="vg", bufs=2, align_bytes=64)
             dst = t[:].rearrange("p g (c i) j -> p g c j i", i=4)
-            src = w2_raw[k][:].rearrange("p g j (c i) -> p g c j i", i=4)
-            n = W2_SHARE[k]
+            src = raw["w2", group][:].rearrange("p g j (c i) -> p g c j i", i=4)
+            n = W2_SHARE[group]
             nc.vector.tensor_copy(out=dst[:, 0:n], in_=src[:, 0:n])
             for g in range(n, total):
                 nc.scalar.copy(out=dst[:, g], in_=src[:, g])
-            w2_grouped[k] = t
-
-        def quant_w2(k):
-            total = len(W2_GROUPS[k]) * G
             codes = ring.tile([P, total, N], U32, name="vc", tag="vc", bufs=2, align_bytes=64)
             scales = ring.tile([P, total, N], U8, name="vs", tag="vs", bufs=2, align_bytes=64)
             nc.vector.quantize_mx(out=codes[:].rearrange("p g n -> p (g n)").bitcast(FP8X4),
                                   scales=scales[:].rearrange("p g n -> p (g n)"),
-                                  in_=w2_grouped[k][:].rearrange("p g n j -> p (g n j)"))
-            for i, e in enumerate(W2_GROUPS[k]):
+                                  in_=t[:].rearrange("p g n j -> p (g n j)"))
+            for i, e in enumerate(group):
                 w2_q[e] = (codes[:, i * G:(i + 1) * G], scales[:, i * G:(i + 1) * G])
 
         y_bank = {}
@@ -196,33 +186,19 @@ def tile_routed_moe_kernel(tc, xT, w1, w2, gate, offs, pos1, pos2, out):
                 else:
                     nc.scalar.copy(out=dst, in_=src)
 
-        for i, group in enumerate(GROUPS):
-            if i + 2 < len(GROUPS):
-                load_w1(GROUPS[i + 2])
-            if i == 2:
-                nc.sync.dma_start(out=pos1_t[:], in_=pos1)
-                nc.sync.dma_start(out=pos2_t[:], in_=pos2)
-            if i + 2 == len(GROUPS) - 1:
-                for k in range(W2_AHEAD):
-                    load_w2(k)
-            for e in group:
-                group_w1(e)
-            for e in group:
-                for g in range(G):
-                    quant_w1(e, g)
-                    hidden(e, g)
-            quant_h(group)
-        for k in range(len(W2_GROUPS)):
-            group_w2(k)
-            if k + W2_AHEAD < len(W2_GROUPS):
-                load_w2(k + W2_AHEAD)
-            if k + W2_AHEAD == len(W2_GROUPS) - 1:
-                for r in range(2):
-                    gate_t[r] = raw_tile([P, T])
-                    nc.sync.dma_start(out=gate_t[r][:], in_=gate[r])
-            quant_w2(k)
-            for e in W2_GROUPS[k]:
-                second(e)
+        for kind, group in ORDER:
+            if kind == "w1":
+                for i, e in enumerate(group):
+                    group_w1(e, raw[kind, group][:, i])
+                for e in group:
+                    for g in range(G):
+                        quant_w1(e, g)
+                        hidden(e, g)
+                quant_h(group)
+            else:
+                prepare_w2(group)
+                for e in group:
+                    second(e)
 
         at = 0
         for i, n in enumerate(OUT_CHUNKS):
@@ -230,8 +206,8 @@ def tile_routed_moe_kernel(tc, xT, w1, w2, gate, offs, pos1, pos2, out):
             part = slice(at // 16, (at + n) // 16)
             a = ring.tile([P, n], F32, name="hg", tag="hg", bufs=3, align_bytes=64)
             b = ring.tile([P, n], F32, name="hg", tag="hg", bufs=3, align_bytes=64)
-            nc.vector.tensor_tensor(a[:], y_all[:].indirect(pos1_t[:, part]), gate_t[0][:, s], MULT)
-            nc.vector.tensor_tensor(b[:], y_all[:].indirect(pos2_t[:, part]), gate_t[1][:, s], MULT)
+            nc.vector.tensor_tensor(a[:], y_all[:].indirect(pos1_t[:, part]), gate_t[:, 0, s], MULT)
+            nc.vector.tensor_tensor(b[:], y_all[:].indirect(pos2_t[:, part]), gate_t[:, 1, s], MULT)
             nc.vector.tensor_tensor(a[:], a[:], b[:], ADD)
             nc.sync.dma_start(out=out[:, s], in_=a[:])
             at += n

@@ -19,11 +19,11 @@ ADD = mybir.AluOpType.add
 P = 128
 J = 4
 G = H // 512
-X_CHUNK = 256
+X_CHUNKS = ((0, 512), (512, 768))
 GATHERS = (512, 512, 512)
-V_SHARE = [(128, 16), (128, 0)] + [(128, 16)] * 7 + [(128, 0), (64, 64), (128, 32)]
+V_SHARE = [(96, 0)] * 3 + [(128, 0)] * 7 + [(96, 16), (128, 32)]
 Y_BANKS = ((0, 1, 2, 3), (4, 5, 6, 7), (8, 9, 10), (11,))
-W2_SHARE = {(0, 1): 3, (2, 3): 3, (4, 5): 4, (6, 7): 2, (8, 9): 4, (10,): 1, (11,): 2}
+W2_SHARE = {(0, 1): 3, (2, 3): 4, (4, 5): 3, (6, 7): 2, (8, 9): 4, (10,): 0, (11,): 1}
 W1_GROUPS = ((0, 1), (2, 3), (4, 5), (6, 7), (8, 9), (10,), (11,))
 ORDER = [("w1", (0, 1)), ("w1", (2, 3)), ("w1", (4, 5)), ("w1", (6, 7)), ("w2", (0, 1)), ("w1", (8, 9)), ("w2", (2, 3)), ("w2", (4, 5)),
          ("w1", (10,)), ("w2", (6, 7)), ("w1", (11,)), ("w2", (8, 9)), ("w2", (10,)), ("w2", (11,))]
@@ -72,21 +72,15 @@ def tile_routed_moe_kernel(tc, xT, w1, w2, gate, offs, pos1, pos2, out):
         x_codes = keep.tile([P, T], U32, name="x_codes", align_bytes=64)
         x_scales = keep.tile([P, T], U8, name="x_scales", align_bytes=64)
         nc.gpsimd.memset(x_scales[:], 0)
-        x_tiles = [ring.tile([P, X_CHUNK, J], BF16, name="hg", tag="hg", bufs=3, align_bytes=64) for b in range(3)]
         x_grouped = []
-        for b in range(T // X_CHUNK):
-            t = x_tiles[b]
-            dst = t[:].rearrange("p (c i) j -> p c j i", i=4)
-            src = x_raw[:, :, b * X_CHUNK:(b + 1) * X_CHUNK].rearrange("p j (c i) -> p c j i", i=4)
-            if b >= 1:
-                nc.scalar.copy(out=dst, in_=src)
-            else:
-                nc.vector.tensor_copy(out=dst, in_=src)
+        for a, b in X_CHUNKS:
+            t = ring.tile([P, b - a, J], BF16, name="hg", tag="hg", bufs=3, align_bytes=64)
+            nc.vector.tensor_copy(out=t[:].rearrange("p (c i) j -> p c j i", i=4),
+                                  in_=x_raw[:, :, a:b].rearrange("p j (c i) -> p c j i", i=4))
             x_grouped.append(t)
-        for b in range(T // X_CHUNK):
-            s = slice(b * X_CHUNK, (b + 1) * X_CHUNK)
-            nc.vector.quantize_mx(out=x_codes[:, s].bitcast(FP8X4), scales=x_scales[:, s],
-                                  in_=x_grouped[b][:].rearrange("p n j -> p (n j)"))
+        for (a, b), t in zip(X_CHUNKS, x_grouped):
+            nc.vector.quantize_mx(out=x_codes[:, a:b].bitcast(FP8X4), scales=x_scales[:, a:b],
+                                  in_=t[:].rearrange("p n j -> p (n j)"))
         slot_codes = {}
         at = 0
         for i, n in enumerate(GATHERS):
@@ -152,7 +146,8 @@ def tile_routed_moe_kernel(tc, xT, w1, w2, gate, offs, pos1, pos2, out):
             dst = t[:].rearrange("p g (c i) j -> p g c j i", i=4)
             src = raw["w2", group][:].rearrange("p g j (c i) -> p g c j i", i=4)
             n = W2_SHARE[group]
-            nc.vector.tensor_copy(out=dst[:, 0:n], in_=src[:, 0:n])
+            if n > 0:
+                nc.vector.tensor_copy(out=dst[:, 0:n], in_=src[:, 0:n])
             for g in range(n, total):
                 nc.scalar.copy(out=dst[:, g], in_=src[:, g])
             codes = ring.tile([P, total, N], U32, name="vc", tag="vc", bufs=2, align_bytes=64)

from contextlib import ExitStack

import concourse.mybir as mybir

K, T, E, C, H, N = 512, 768, 12, 128, 1024, 128
FLOPS = 2 * E * C * H * (K + N)

F32 = mybir.dt.float32
BF16 = mybir.dt.bfloat16
U32 = mybir.dt.uint32
I32 = mybir.dt.int32
U16 = mybir.dt.uint16
U8 = mybir.dt.uint8
FP8X4 = mybir.dt.float8_e4m3fn_x4
SILU = mybir.ActivationFunctionType.Silu
MULT = mybir.AluOpType.mult
ADD = mybir.AluOpType.add

P = 128
J = 4
G = H // 512
X_CHUNKS = ((0, 512), (512, 768))
GATHERS = (512, 512, 512)
V_SHARE = [(96, 0)] * 3 + [(128, 0)] * 7 + [(96, 16), (128, 32)]
Y_BANKS = ((0, 1, 2, 3), (4, 5, 6, 7), (8, 9, 10), (11,))
W2_SHARE = {(0, 1): 3, (2, 3): 4, (4, 5): 3, (6, 7): 2, (8, 9): 4, (10,): 0, (11,): 1}
W1_GROUPS = ((0, 1), (2, 3), (4, 5), (6, 7), (8, 9), (10,), (11,))
ORDER = [("w1", (0, 1)), ("w1", (2, 3)), ("w1", (4, 5)), ("w1", (6, 7)), ("w2", (0, 1)), ("w1", (8, 9)), ("w2", (2, 3)), ("w2", (4, 5)),
         ("w1", (10,)), ("w2", (6, 7)), ("w1", (11,)), ("w2", (8, 9)), ("w2", (10,)), ("w2", (11,))]
OUT_CHUNKS = (512, 256)
RAW_BUFS = 4


def tile_routed_moe_kernel(tc, xT, w1, w2, gate, offs, pos1, pos2, out):
    nc = tc.nc
    with ExitStack() as ctx:
        keep = ctx.enter_context(tc.tile_pool(name="keep", bufs=1))
        ring = ctx.enter_context(tc.tile_pool(name="ring", bufs=2))
        psum = ctx.enter_context(tc.psum_pool(name="psum", bufs=2))

        offs_t = keep.tile([P, E * C // 16], U16, name="offs_t")
        pos1_t = keep.tile([P, T // 16], U16, name="pos1_t")
        pos2_t = keep.tile([P, T // 16], U16, name="pos2_t")
        y_all = keep.tile([P, E * C], F32, name="y_all")
        warm = keep.tile([P, 2], F32, name="warm")

        nc.vector.memset(warm[:], 0.0)
        nc.scalar.activation(warm[:, 1:2], warm[:, 0:1], SILU)

        def raw_tile(shape):
            return ring.tile(shape, F32, name="raw", tag="raw", bufs=RAW_BUFS, align_bytes=64)

        x_raw = raw_tile([P, J, T])
        nc.sync.dma_start(out=x_raw[:], in_=xT.rearrange("(p j) n -> p j n", j=J))
        nc.sync.dma_start(out=offs_t[:], in_=offs)
        raw = {}
        for i, (kind, group) in enumerate(ORDER):
            n = len(group)
            if kind == "w1":
                t = raw_tile([P, n, J, H])
                nc.sync.dma_start(out=t[:], in_=w1[group[0]:group[0] + n].rearrange("e (p j) h -> p e j h", j=J))
            else:
                t = raw_tile([P, n * G, J, N])
                nc.sync.dma_start(out=t[:], in_=w2[group[0]:group[0] + n].rearrange("e (g p j) n -> p (e g) j n", p=P, j=J))
            raw[kind, group] = t
            if i == RAW_BUFS - 2:
                nc.sync.dma_start(out=pos1_t[:], in_=pos1)
                nc.sync.dma_start(out=pos2_t[:], in_=pos2)
        gate_t = raw_tile([P, 2, T])
        nc.sync.dma_start(out=gate_t[:], in_=gate.rearrange("r p t -> p r t"))

        x_codes = keep.tile([P, T], U32, name="x_codes", align_bytes=64)
        x_scales = keep.tile([P, T], U8, name="x_scales", align_bytes=64)
        nc.gpsimd.memset(x_scales[:], 0)
        x_grouped = []
        for a, b in X_CHUNKS:
            t = ring.tile([P, b - a, J], BF16, name="hg", tag="hg", bufs=3, align_bytes=64)
            nc.vector.tensor_copy(out=t[:].rearrange("p (c i) j -> p c j i", i=4),
                                  in_=x_raw[:, :, a:b].rearrange("p j (c i) -> p c j i", i=4))
            x_grouped.append(t)
        for (a, b), t in zip(X_CHUNKS, x_grouped):
            nc.vector.quantize_mx(out=x_codes[:, a:b].bitcast(FP8X4), scales=x_scales[:, a:b],
                                  in_=t[:].rearrange("p n j -> p (n j)"))
        slot_codes = {}
        at = 0
        for i, n in enumerate(GATHERS):
            codes = keep.tile([P, n], U32, name="g_codes%d" % i, align_bytes=64)
            scales = keep.tile([P, n], U8, name="g_scales%d" % i, align_bytes=64)
            part = offs_t[:, at // 16:(at + n) // 16]
            nc.vector.tensor_copy(out=codes[:], in_=x_codes[:].indirect(part))
            nc.vector.tensor_copy(out=scales[:], in_=x_scales[:].indirect(part))
            for q in range(n // C):
                slot_codes[(at + q * C) // C] = (codes[:, q * C:(q + 1) * C], scales[:, q * C:(q + 1) * C])
            at += n

        w1_grouped = {}
        w1_q = {}
        w2_q = {}
        h_grouped = {}
        h_q = {}

        def group_w1(e, raw_e):
            w1_grouped[e] = [ring.tile([P, 4, 128, J], BF16, name="wg", tag="wg", bufs=5, align_bytes=64) for g in range(G)]
            for g in (1, 0):
                dst = w1_grouped[e][g][:].rearrange("p t m j -> p m j t")
                src = raw_e[:, :, g * 512:(g + 1) * 512].rearrange("p j (m t) -> p m j t", t=4)
                m = V_SHARE[e][g]
                if m > 0:
                    nc.vector.tensor_copy(out=dst[:, 0:m], in_=src[:, 0:m])
                if m < 128:
                    nc.scalar.copy(out=dst[:, m:128], in_=src[:, m:128])

        def quant_w1(e, g):
            codes = ring.tile([P, 512], U32, name="wc", tag="wc", bufs=6, align_bytes=64)[:]
            scales = ring.tile([P, 512], U8, name="ws", tag="ws", bufs=6, align_bytes=64)[:]
            nc.vector.quantize_mx(out=codes.bitcast(FP8X4), scales=scales,
                                  in_=w1_grouped[e][g][:].rearrange("p t m j -> p (t m j)"))
            w1_q[e, g] = (codes, scales)

        def hidden(e, g):
            xc, xs = slot_codes[e]
            group = [b for b in W1_GROUPS if e in b][0]
            if group not in h_grouped:
                h_grouped[group] = ring.tile([P, 2, G, C, J], BF16, name="hg", tag="hg", bufs=3, align_bytes=64)
            codes, scales = w1_q[e, g]
            acc = psum.tile([P, 4, C], F32, name="acc", tag="acc", bufs=4)
            for q in range(4):
                s = slice(q * 128, (q + 1) * 128)
                nc.tensor.matmul_mx(out=acc[:, q, :], lhsT=codes[:, s].bitcast(FP8X4), lhsT_scale=scales[:, s],
                                    rhs=xc.bitcast(FP8X4), rhs_scale=xs, start=True, stop=True)
            nc.scalar.activation(h_grouped[group][:, e - group[0], g, :, :], acc[:].rearrange("p t n -> p n t"), SILU)

        def quant_h(group):
            n = len(group)
            codes = keep.tile([P, n, G * C], U32, name="hc%d" % group[0], align_bytes=64)
            scales = keep.tile([P, n, G * C], U8, name="hs%d" % group[0], align_bytes=64)
            nc.vector.quantize_mx(out=codes[:].rearrange("p e n -> p (e n)").bitcast(FP8X4),
                                  scales=scales[:].rearrange("p e n -> p (e n)"),
                                  in_=h_grouped[group][:, 0:n].rearrange("p e g n j -> p (e g n j)"))
            for e in group:
                h_q[e] = (codes[:, e - group[0]], scales[:, e - group[0]])

        def prepare_w2(group):
            total = len(group) * G
            t = ring.tile([P, total, N, J], BF16, name="vg", tag="vg", bufs=2, align_bytes=64)
            dst = t[:].rearrange("p g (c i) j -> p g c j i", i=4)
            src = raw["w2", group][:].rearrange("p g j (c i) -> p g c j i", i=4)
            n = W2_SHARE[group]
            if n > 0:
                nc.vector.tensor_copy(out=dst[:, 0:n], in_=src[:, 0:n])
            for g in range(n, total):
                nc.scalar.copy(out=dst[:, g], in_=src[:, g])
            codes = ring.tile([P, total, N], U32, name="vc", tag="vc", bufs=2, align_bytes=64)
            scales = ring.tile([P, total, N], U8, name="vs", tag="vs", bufs=2, align_bytes=64)
            nc.vector.quantize_mx(out=codes[:].rearrange("p g n -> p (g n)").bitcast(FP8X4),
                                  scales=scales[:].rearrange("p g n -> p (g n)"),
                                  in_=t[:].rearrange("p g n j -> p (g n j)"))
            for i, e in enumerate(group):
                w2_q[e] = (codes[:, i * G:(i + 1) * G], scales[:, i * G:(i + 1) * G])

        y_bank = {}

        def second(e):
            wc, ws = w2_q[e]
            hc, hs = h_q[e]
            bank = [b for b in Y_BANKS if e in b][0]
            if e == bank[0]:
                y_bank[bank] = psum.tile([N, 4, C], F32, name="acc_y", tag="acc_y", bufs=4)
            acc = y_bank[bank]
            for g in range(G):
                s = slice(g * C, (g + 1) * C)
                nc.tensor.matmul_mx(out=acc[:, e - bank[0], :], lhsT=wc[:, g, :].bitcast(FP8X4), lhsT_scale=ws[:, g, :],
                                    rhs=hc[:, s].bitcast(FP8X4), rhs_scale=hs[:, s],
                                    start=(g == 0), stop=(g == G - 1))
            if e == bank[-1]:
                n = len(bank)
                dst = y_all[:, bank[0] * C:(e + 1) * C]
                src = acc[:, 0:n, :].rearrange("p a n -> p (a n)")
                if e == E - 1:
                    nc.vector.tensor_copy(out=dst, in_=src)
                else:
                    nc.scalar.copy(out=dst, in_=src)

        for kind, group in ORDER:
            if kind == "w1":
                for i, e in enumerate(group):
                    group_w1(e, raw[kind, group][:, i])
                for e in group:
                    for g in range(G):
                        quant_w1(e, g)
                        hidden(e, g)
                quant_h(group)
            else:
                prepare_w2(group)
                for e in group:
                    second(e)

        at = 0
        for i, n in enumerate(OUT_CHUNKS):
            s = slice(at, at + n)
            part = slice(at // 16, (at + n) // 16)
            a = ring.tile([P, n], F32, name="hg", tag="hg", bufs=3, align_bytes=64)
            b = ring.tile([P, n], F32, name="hg", tag="hg", bufs=3, align_bytes=64)
            nc.vector.tensor_tensor(a[:], y_all[:].indirect(pos1_t[:, part]), gate_t[:, 0, s], MULT)
            nc.vector.tensor_tensor(b[:], y_all[:].indirect(pos2_t[:, part]), gate_t[:, 1, s], MULT)
            nc.vector.tensor_tensor(a[:], a[:], b[:], ADD)
            nc.sync.dma_start(out=out[:, s], in_=a[:])
            at += n
